import numpy as np
import ml_dtypes


def mxq(x, axis, fmt="e4m3"):
    dtype, down = {"e4m3": (ml_dtypes.float8_e4m3fn, 7), "e5m2": (ml_dtypes.float8_e5m2, 14)}[fmt]
    v = np.moveaxis(np.asarray(x, np.float32).astype(ml_dtypes.bfloat16).astype(np.float64), axis, -1)
    blocks = v.reshape(v.shape[:-1] + (-1, 32))
    amax = np.abs(blocks).max(-1, keepdims=True)
    byte = np.maximum(np.where(amax > 0, np.frexp(amax)[1] - 1 + 127, 0) - down, 1)
    scale = np.exp2(byte - 127.0)
    codes = (blocks / scale).astype(np.float32).astype(dtype).astype(np.float64)
    return np.moveaxis((codes * scale).reshape(v.shape), -1, axis)


WIDE = False


def mx_kscale(k):
    if not WIDE:
        return np.ones(k)
    levels = np.array([10, -10, 5, -5, 0])
    if k % 512:
        return np.exp2(np.random.permutation(np.resize(levels, k // 32))).repeat(32)
    a = np.empty((k // 512, 16))
    for p in range(k // 512):
        a[p, :8] = np.random.permutation(np.resize(levels, 8))
        for g in range(8):
            far = levels[np.abs(levels - a[p, g]) >= 10]
            a[p, g + 8] = far[np.random.randint(len(far))]
    return np.exp2(a.ravel()).repeat(32)


def f64(x):
    return np.asarray(x).astype(np.float64)


def striped(idx):
    return np.tile(idx.reshape(-1, 16).T, (8, 1)).astype(np.uint16)


def unstriped(offs):
    return offs[:16].T.reshape(-1).astype(np.int64)


def striped8(idx):
    return np.concatenate([x.reshape(-1, 16).T for x in idx]).astype(np.uint16)


def runs(offs, k):
    lists = np.stack([offs[16 * r : 16 * r + 16].T.reshape(-1) for r in range(8)]).astype(np.int64)
    return lists[np.arange(k) % 512 // 64]


def pack_weight(w):
    k, n = w.shape
    w = f64(np.asarray(w, np.float32).astype(ml_dtypes.bfloat16)).reshape(k // 32, 32, n)
    amax = np.abs(w).max(1)
    byte = np.clip(np.where(amax > 0, np.frexp(amax)[1] - 1 + 127 - 7, 1), 1, 254)
    scaled = (w * np.exp2(127.0 - byte)[:, None, :]).reshape(k, n).astype(np.float32)
    words = np.ascontiguousarray(scaled.reshape(k // 512, 128, 4, n).transpose(0, 1, 3, 2)).astype(ml_dtypes.float8_e4m3fn).view(np.uint8)
    return words, np.ascontiguousarray(byte.astype(np.uint8).reshape(k // 512, 16, n))


def unpack_weight(words, scales):
    g, p, n, _ = words.shape
    vals = np.ascontiguousarray(words).view(ml_dtypes.float8_e4m3fn).astype(np.float64) * np.repeat(np.exp2(scales.astype(np.float64) - 127.0), 8, axis=1)[..., None]
    return vals.transpose(0, 1, 3, 2).reshape(g * 512, n)


def sigmoid(v):
    return 1.0 / (1.0 + np.exp(-np.maximum(v, -700.0)))


K, T, S, N, H, W = 512, 2048, 512, 512, 512, 256


def setup_inputs():
    n = np.random.standard_normal
    s = mx_kscale(K)[:, None]
    u = mx_kscale(S)
    packed_xT = pack_weight(n((K, T)) * s)
    perm = np.random.permutation(H)
    return {
        "x_words": packed_xT[0],
        "x_scales": packed_xT[1],
        "wa": (n((K, H)) / np.sqrt(K) / s).astype(np.float32),
        "gt": (np.random.uniform(0.5, 1.5, (S, 1)) * u[:, None]).astype(np.float32),
        "w1": (n((S, H)) / np.sqrt(S) / u[:, None]).astype(np.float32),
        "gp": (np.random.uniform(0.5, 1.5, (H, 1)) * u[:, None]).astype(np.float32),
        "res": (1.5 * n((N, H))).astype(np.float32),
        "w2": (n((H, N)) / np.sqrt(H) / u[:, None]).astype(np.float32),
        "offs": striped(np.random.permutation(T)[:S]),
        "n1": striped(perm[:W]),
        "n2": striped(perm[W:]),
        "n3": striped8(np.stack([np.random.permutation(H) for _ in range(8)])),
    }


def reference(x_words, x_scales, wa, gt, w1, gp, res, w2, offs, n1, n2, n3):
    xq = unpack_weight(x_words, x_scales)[:, unstriped(offs)]
    y = xq.T @ mxq(f64(wa), 0, "e4m3")
    pa = y[:, unstriped(n1)]
    pb = y[:, unstriped(n2)]
    ra = pa * sigmoid(pb)
    ds = y.copy()
    ds[:, unstriped(n2)] = ra
    z = f64(gt) * ds
    h = mxq(f64(w1), 0, "e4m3").T @ mxq(z, 0, "e4m3")
    z2 = f64(gp) * (h - (h[np.arange(H)[:, None], runs(n3, H)]))
    return f64(res) + (mxq(f64(w2), 0, "e4m3").T @ mxq(z2, 0, "e4m3"))

@@ -1,0 +1,192 @@
+from contextlib import ExitStack
+
+import concourse.mybir as mybir
+
+K, T, S, N, H, W = 512, 2048, 512, 512, 512, 256
+FLOPS = 3 * 2 * 512 * 512 * 512
+
+F32 = mybir.dt.float32
+BF16 = mybir.dt.bfloat16
+I32 = mybir.dt.int32
+U32 = mybir.dt.uint32
+U16 = mybir.dt.uint16
+U8 = mybir.dt.uint8
+FP8X4 = mybir.dt.float8_e4m3fn_x4
+ACT = mybir.ActivationFunctionType
+ALU = mybir.AluOpType
+
+P = 128
+PACK = 4
+HALF = 256
+CHUNK = 128
+
+
+def tile_picked_tok2folddif_none_p_kernel(
+    tc, x_words, x_scales, wa, gt, w1, gp, res, w2, offs, n1, n2, n3, out
+):
+    nc = tc.nc
+    with ExitStack() as ctx:
+        lists = ctx.enter_context(tc.tile_pool(name="lists", bufs=1))
+        keep = ctx.enter_context(tc.tile_pool(name="keep", bufs=1))
+        psum = ctx.enter_context(tc.psum_pool(name="psum", bufs=1))
+
+        def sb(name, shape, dtype, tag=None):
+            return keep.tile(shape, dtype, name=name, tag=tag or name, align_bytes=64)
+
+        def rows4(w):
+            return w.rearrange("(p j) c -> p j c", j=PACK)
+
+        def quantize(codes, scales, values):
+            nc.vector.quantize_mx(out=codes.bitcast(FP8X4), scales=scales, in_=values)
+
+        def product(acc, lhs, lhs_scales, rhs, rhs_scales):
+            nc.tensor.matmul_mx(
+                out=acc, lhsT=lhs.bitcast(FP8X4), lhsT_scale=lhs_scales,
+                rhs=rhs.bitcast(FP8X4), rhs_scale=rhs_scales, start=True, stop=True,
+            )
+
+        def weave_views(dst, src):
+            return (
+                dst.rearrange("p (c i j) -> p c j i", i=PACK, j=PACK),
+                src.rearrange("p j (c i) -> p c j i", i=PACK),
+            )
+
+        xw = sb("xw", [P, T], U32)
+        xs = sb("xs", [P, T], U8)
+        xs_in = sb("xs_in", [P, T], U8)
+        for q in range(4):
+            nc.sync.dma_start(
+                xs_in[32 * q : 32 * q + 4, :].bitcast(I32), x_scales[0, 4 * q : 4 * q + 4, :].bitcast(I32)
+            )
+        nc.sync.dma_start(xw[:].bitcast(I32), x_words[0].rearrange("p c r -> p (c r)").bitcast(I32))
+        nc.vector.memset(xs[:].bitcast(I32), 0)
+        for q in range(4):
+            rows = slice(32 * q, 32 * q + 4)
+            nc.vector.tensor_copy(xs[rows, :].bitcast(I32), xs_in[rows, :].bitcast(I32))
+        offs_t = lists.tile([P, S // 16], U16, name="offs_t")
+        nc.sync.dma_start(offs_t[:], offs)
+        wa_raw = [sb(f"wa_raw{h}", [P, PACK, HALF], F32) for h in range(2)]
+        for h in range(2):
+            nc.sync.dma_start(wa_raw[h][:], rows4(wa)[:, :, h * HALF : (h + 1) * HALF])
+        gt_t = sb("gt_t", [P, PACK], F32)
+        gp_t = sb("gp_t", [P, PACK], F32)
+        n1_t = lists.tile([P, W // 16], U16, name="n1_t")
+        n2_t = lists.tile([P, W // 16], U16, name="n2_t")
+        n3_t = lists.tile([P, H // 16], U16, name="n3_t")
+        nc.sync.dma_start(n1_t[:], n1)
+        nc.sync.dma_start(n2_t[:], n2)
+        w1_raw = sb("w1_raw", [P, PACK, H], F32)
+        nc.sync.dma_start(w1_raw[:], rows4(w1))
+        nc.sync.dma_start(gt_t[:], gt.rearrange("(p j) o -> p (j o)", j=PACK))
+        nc.sync.dma_start(n3_t[:], n3)
+        nc.sync.dma_start(gp_t[:], gp.rearrange("(p j) o -> p (j o)", j=PACK))
+        w2_raw = sb("w2_raw", [P, PACK, N], F32)
+        nc.sync.dma_start(w2_raw[:], rows4(w2))
+        res_t = sb("res_t", [P, PACK, H], F32)
+        nc.sync.dma_start(res_t[:], res.rearrange("(m p) c -> p m c", p=P))
+
+        tok_scales = sb("tok_scales", [P, S], U8)
+        tok_words = sb("tok_words", [P, S], U32)
+        nc.vector.tensor_copy(tok_scales[:].rearrange("p (t m) -> p m t", t=PACK), xs[:].indirect(offs_t[:]))
+        nc.vector.tensor_copy(tok_words[:].rearrange("p (t m) -> p m t", t=PACK), xw[:].indirect(offs_t[:]))
+
+        y_ps = [psum.tile([P, H], F32, name=f"y_ps{t}", tag=f"bank{t}") for t in range(PACK)]
+        wa_mx = []
+        for h in range(2):
+            wa_bf = sb(f"wa_bf{h}", [P, PACK * HALF], BF16)
+            dst, src = weave_views(wa_bf[:], wa_raw[h][:])
+            if h == 0:
+                nc.scalar.copy(dst, src)
+            else:
+                nc.vector.tensor_copy(dst, src)
+            wa_codes = sb(f"wa_codes{h}", [P, HALF], U32)
+            wa_scales = sb(f"wa_scales{h}", [P, HALF], U8)
+            quantize(wa_codes[:], wa_scales[:], wa_bf[:])
+            wa_mx.append((wa_codes, wa_scales))
+        for t in range(PACK):
+            cols = slice(t * P, (t + 1) * P)
+            for h in range(2):
+                product(y_ps[t][:, h * HALF : (h + 1) * HALF], tok_words[:, cols], tok_scales[:, cols],
+                        wa_mx[h][0][:], wa_mx[h][1][:])
+
+        ds = [sb(f"ds{t}", [P, H], F32) for t in range(PACK)]
+        for t in range(3):
+            nc.vector.tensor_copy(ds[t][:], y_ps[t][:])
+        z_rows = sb("z_rows", [P, PACK, H], BF16)
+        for t in range(PACK):
+            pa = sb(f"pa{t}", [P, W], F32)
+            sig = sb(f"sig{t}", [P, W], F32)
+            nc.scalar.activation(sig[:], ds[t][:].indirect(n2_t[:]), ACT.Sigmoid)
+            nc.scalar.activation(pa[:], ds[t][:].indirect(n1_t[:]), ACT.Copy)
+            if t == 0:
+                nc.scalar.copy(ds[3][:], y_ps[3][:])
+            nc.vector.tensor_tensor(ds[t][:].indirect(n2_t[:]), pa[:], sig[:], ALU.mult)
+            nc.vector.tensor_scalar(z_rows[:, t, :], ds[t][:], gt_t[:, t : t + 1], None, ALU.mult)
+
+        w1_bf = sb("w1_bf", [P, PACK * H], BF16, tag="pa1")
+        nc.scalar.copy(
+            w1_bf[:].rearrange("p (t m j) -> p m j t", t=PACK, j=PACK),
+            w1_raw[:].rearrange("p j (m t) -> p m j t", t=PACK),
+        )
+        w1_codes = sb("w1_codes", [P, H], U32)
+        w1_scales = sb("w1_scales", [P, H], U8)
+        quantize(w1_codes[:], w1_scales[:], w1_bf[:])
+
+        h_ps = [psum.tile([P, H], F32, name=f"h_ps{t}", tag=f"bank{PACK + t}") for t in range(PACK)]
+        z_mx = []
+        for h in range(2):
+            z_bf = sb(f"z_bf{h}", [P, PACK * HALF], BF16, tag="pa1" if h == 0 else None)
+            dst, src = weave_views(z_bf[:], z_rows[:, :, h * HALF : (h + 1) * HALF])
+            if h == 0:
+                nc.vector.tensor_copy(dst, src)
+            else:
+                nc.scalar.copy(dst, src)
+            z_codes = sb(f"z_codes{h}", [P, HALF], U32)
+            z_scales = sb(f"z_scales{h}", [P, HALF], U8)
+            quantize(z_codes[:], z_scales[:], z_bf[:])
+            z_mx.append((z_codes, z_scales))
+        for t in range(PACK):
+            cols = slice(t * P, (t + 1) * P)
+            for h in range(2):
+                product(h_ps[t][:, h * HALF : (h + 1) * HALF], w1_codes[:, cols], w1_scales[:, cols],
+                        z_mx[h][0][:], z_mx[h][1][:])
+
+        w2_codes = sb("w2_codes", [P, N], U32, tag="z_bf1")
+        w2_scales = sb("w2_scales", [P, N], U8)
+        for h in range(2):
+            cols = slice(h * HALF, (h + 1) * HALF)
+            w2_bf = sb(f"w2_bf{h}", [P, PACK * HALF], BF16, tag="pa2" if h == 0 else "z_rows")
+            dst, src = weave_views(w2_bf[:], w2_raw[:, :, cols])
+            nc.scalar.copy(dst, src)
+            quantize(w2_codes[:, cols], w2_scales[:, cols], w2_bf[:])
+
+        hs = [sb(f"hs{t}", [P, H], F32) for t in range(PACK)]
+        for t in range(PACK):
+            if t != 1:
+                nc.vector.tensor_scalar(hs[t][:], h_ps[t][:], gp_t[:, t : t + 1], None, ALU.mult)
+            else:
+                nc.scalar.activation(hs[t][:], h_ps[t][:], ACT.Copy, scale=gp_t[:, t : t + 1])
+
+        out_rows = out.rearrange("(m p) c -> p m c", p=P)
+        for c in range(H // CHUNK):
+            cols = slice(c * CHUNK, (c + 1) * CHUNK)
+            hg = sb(f"hg{c}", [P, PACK, CHUNK], F32)
+            z2_rows = sb(f"z2_rows{c}", [P, PACK, CHUNK], BF16)
+            for t in range(PACK):
+                nc.scalar.activation(
+                    hg[:, t, :], hs[t][:].indirect(n3_t[:, c * CHUNK // 16 : (c + 1) * CHUNK // 16]), ACT.Copy
+                )
+                nc.vector.tensor_tensor(z2_rows[:, t, :], hs[t][:, cols], hg[:, t, :], ALU.subtract)
+            z2_bf = sb(f"z2_bf{c}", [P, PACK * CHUNK], BF16)
+            dst, src = weave_views(z2_bf[:], z2_rows[:])
+            nc.vector.tensor_copy(dst, src)
+            z2_codes = sb(f"z2_codes{c}", [P, CHUNK], U32)
+            z2_scales = sb(f"z2_scales{c}", [P, CHUNK], U8)
+            quantize(z2_codes[:], z2_scales[:], z2_bf[:])
+            out_ps = psum.tile([P, PACK, CHUNK], F32, name=f"out_ps{c}", tag=f"bank{c}")
+            for m in range(PACK):
+                rows = slice(m * P, (m + 1) * P)
+                product(out_ps[:, m, :], w2_codes[:, rows], w2_scales[:, rows], z2_codes[:], z2_scales[:])
+            out_sb = sb(f"out_sb{c}", [P, PACK, CHUNK], F32)
+            nc.vector.tensor_tensor(out_sb[:], out_ps[:], res_t[:, :, cols], ALU.add)
+            nc.sync.dma_start(out_rows[:, :, cols], out_sb[:])

@@ -18,7 +18,8 @@ ALU = mybir.AluOpType
 P = 128
 PACK = 4
 HALF = 256
-CHUNK = 128
+Z_SPLIT = 320
+W2_SPLIT = 384
 
 
 def tile_picked_tok2folddif_none_p_kernel(
@@ -59,12 +60,12 @@ def tile_picked_tok2folddif_none_p_kernel(
                 xs_in[32 * q : 32 * q + 4, :].bitcast(I32), x_scales[0, 4 * q : 4 * q + 4, :].bitcast(I32)
             )
         nc.sync.dma_start(xw[:].bitcast(I32), x_words[0].rearrange("p c r -> p (c r)").bitcast(I32))
+        offs_t = lists.tile([P, S // 16], U16, name="offs_t")
+        nc.sync.dma_start(offs_t[:], offs)
         nc.vector.memset(xs[:].bitcast(I32), 0)
         for q in range(4):
             rows = slice(32 * q, 32 * q + 4)
             nc.vector.tensor_copy(xs[rows, :].bitcast(I32), xs_in[rows, :].bitcast(I32))
-        offs_t = lists.tile([P, S // 16], U16, name="offs_t")
-        nc.sync.dma_start(offs_t[:], offs)
         wa_raw = [sb(f"wa_raw{h}", [P, PACK, HALF], F32) for h in range(2)]
         for h in range(2):
             nc.sync.dma_start(wa_raw[h][:], rows4(wa)[:, :, h * HALF : (h + 1) * HALF])
@@ -75,13 +76,13 @@ def tile_picked_tok2folddif_none_p_kernel(
         n3_t = lists.tile([P, H // 16], U16, name="n3_t")
         nc.sync.dma_start(n1_t[:], n1)
         nc.sync.dma_start(n2_t[:], n2)
-        w1_raw = sb("w1_raw", [P, PACK, H], F32)
-        nc.sync.dma_start(w1_raw[:], rows4(w1))
-        nc.sync.dma_start(gt_t[:], gt.rearrange("(p j) o -> p (j o)", j=PACK))
-        nc.sync.dma_start(n3_t[:], n3)
-        nc.sync.dma_start(gp_t[:], gp.rearrange("(p j) o -> p (j o)", j=PACK))
         w2_raw = sb("w2_raw", [P, PACK, N], F32)
         nc.sync.dma_start(w2_raw[:], rows4(w2))
+        nc.sync.dma_start(gt_t[:], gt.rearrange("(p j) o -> p (j o)", j=PACK))
+        w1_raw = sb("w1_raw", [P, PACK, H], F32)
+        nc.sync.dma_start(w1_raw[:], rows4(w1))
+        nc.sync.dma_start(n3_t[:], n3)
+        nc.sync.dma_start(gp_t[:], gp.rearrange("(p j) o -> p (j o)", j=PACK))
         res_t = sb("res_t", [P, PACK, H], F32)
         nc.sync.dma_start(res_t[:], res.rearrange("(m p) c -> p m c", p=P))
 
@@ -112,7 +113,6 @@ def tile_picked_tok2folddif_none_p_kernel(
         ds = [sb(f"ds{t}", [P, H], F32) for t in range(PACK)]
         for t in range(3):
             nc.vector.tensor_copy(ds[t][:], y_ps[t][:])
-        z_rows = sb("z_rows", [P, PACK, H], BF16)
         for t in range(PACK):
             pa = sb(f"pa{t}", [P, W], F32)
             sig = sb(f"sig{t}", [P, W], F32)
@@ -121,29 +121,31 @@ def tile_picked_tok2folddif_none_p_kernel(
             if t == 0:
                 nc.scalar.copy(ds[3][:], y_ps[3][:])
             nc.vector.tensor_tensor(ds[t][:].indirect(n2_t[:]), pa[:], sig[:], ALU.mult)
-            nc.vector.tensor_scalar(z_rows[:, t, :], ds[t][:], gt_t[:, t : t + 1], None, ALU.mult)
 
         w1_bf = sb("w1_bf", [P, PACK * H], BF16, tag="pa1")
         nc.scalar.copy(
             w1_bf[:].rearrange("p (t m j) -> p m j t", t=PACK, j=PACK),
             w1_raw[:].rearrange("p j (m t) -> p m j t", t=PACK),
         )
+        z_rows = sb("z_rows", [P, PACK, H], BF16, tag="sig1")
+        nc.vector.tensor_scalar(z_rows[:, 3, :], ds[3][:], gt_t[:, 3:4], None, ALU.mult)
+        for t in range(3):
+            nc.scalar.activation(z_rows[:, t, :], ds[t][:], ACT.Copy, scale=gt_t[:, t : t + 1])
         w1_codes = sb("w1_codes", [P, H], U32)
         w1_scales = sb("w1_scales", [P, H], U8)
         quantize(w1_codes[:], w1_scales[:], w1_bf[:])
 
         h_ps = [psum.tile([P, H], F32, name=f"h_ps{t}", tag=f"bank{PACK + t}") for t in range(PACK)]
+        z_bf = sb("z_bf", [P, PACK * H], BF16, tag="pa1")
+        dst, src = weave_views(z_bf[:, : PACK * Z_SPLIT], z_rows[:, :, :Z_SPLIT])
+        nc.vector.tensor_copy(dst, src)
+        dst, src = weave_views(z_bf[:, PACK * Z_SPLIT :], z_rows[:, :, Z_SPLIT:])
+        nc.scalar.copy(dst, src)
         z_mx = []
         for h in range(2):
-            z_bf = sb(f"z_bf{h}", [P, PACK * HALF], BF16, tag="pa1" if h == 0 else None)
-            dst, src = weave_views(z_bf[:], z_rows[:, :, h * HALF : (h + 1) * HALF])
-            if h == 0:
-                nc.vector.tensor_copy(dst, src)
-            else:
-                nc.scalar.copy(dst, src)
             z_codes = sb(f"z_codes{h}", [P, HALF], U32)
             z_scales = sb(f"z_scales{h}", [P, HALF], U8)
-            quantize(z_codes[:], z_scales[:], z_bf[:])
+            quantize(z_codes[:], z_scales[:], z_bf[:, h * PACK * HALF : (h + 1) * PACK * HALF])
             z_mx.append((z_codes, z_scales))
         for t in range(PACK):
             cols = slice(t * P, (t + 1) * P)
@@ -151,14 +153,15 @@ def tile_picked_tok2folddif_none_p_kernel(
                 product(h_ps[t][:, h * HALF : (h + 1) * HALF], w1_codes[:, cols], w1_scales[:, cols],
                         z_mx[h][0][:], z_mx[h][1][:])
 
-        w2_codes = sb("w2_codes", [P, N], U32, tag="z_bf1")
+        w2_codes = sb("w2_codes", [P, N], U32, tag="sig1")
         w2_scales = sb("w2_scales", [P, N], U8)
-        for h in range(2):
-            cols = slice(h * HALF, (h + 1) * HALF)
-            w2_bf = sb(f"w2_bf{h}", [P, PACK * HALF], BF16, tag="pa2" if h == 0 else "z_rows")
-            dst, src = weave_views(w2_bf[:], w2_raw[:, :, cols])
-            nc.scalar.copy(dst, src)
-            quantize(w2_codes[:, cols], w2_scales[:, cols], w2_bf[:])
+        for part, (cols, tag) in enumerate(((slice(0, W2_SPLIT), "wa_bf1"), (slice(W2_SPLIT, N), "pa1"))):
+            width = cols.stop - cols.start
+            w2_bf = sb(f"w2_bf{part}", [P, width, PACK], BF16, tag=tag)
+            nc.gpsimd.tensor_scalar(
+                w2_bf[:], w2_raw[:, :, cols].rearrange("p j c -> p c j"), 1.0, 0.0, ALU.mult, ALU.add
+            )
+            quantize(w2_codes[:, cols], w2_scales[:, cols], w2_bf[:].rearrange("p c j -> p (c j)"))
 
         hs = [sb(f"hs{t}", [P, H], F32) for t in range(PACK)]
         for t in range(PACK):
@@ -168,25 +171,38 @@ def tile_picked_tok2folddif_none_p_kernel(
                 nc.scalar.activation(hs[t][:], h_ps[t][:], ACT.Copy, scale=gp_t[:, t : t + 1])
 
         out_rows = out.rearrange("(m p) c -> p m c", p=P)
-        for c in range(H // CHUNK):
-            cols = slice(c * CHUNK, (c + 1) * CHUNK)
-            hg = sb(f"hg{c}", [P, PACK, CHUNK], F32)
-            z2_rows = sb(f"z2_rows{c}", [P, PACK, CHUNK], BF16)
+        def second_difference(c, cols, hg_tag):
+            width = cols.stop - cols.start
+            hg = sb(f"hg{c}", [P, PACK, width], F32, tag=hg_tag)
+            z2_rows = sb(f"z2_rows{c}", [P, PACK, width], BF16)
             for t in range(PACK):
                 nc.scalar.activation(
-                    hg[:, t, :], hs[t][:].indirect(n3_t[:, c * CHUNK // 16 : (c + 1) * CHUNK // 16]), ACT.Copy
+                    hg[:, t, :], hs[t][:].indirect(n3_t[:, cols.start // 16 : cols.stop // 16]), ACT.Copy
                 )
                 nc.vector.tensor_tensor(z2_rows[:, t, :], hs[t][:, cols], hg[:, t, :], ALU.subtract)
-            z2_bf = sb(f"z2_bf{c}", [P, PACK * CHUNK], BF16)
-            dst, src = weave_views(z2_bf[:], z2_rows[:])
-            nc.vector.tensor_copy(dst, src)
-            z2_codes = sb(f"z2_codes{c}", [P, CHUNK], U32)
-            z2_scales = sb(f"z2_scales{c}", [P, CHUNK], U8)
+            z2_bf = sb(f"z2_bf{c}", [P, PACK * width], BF16)
+            nc.vector.tensor_copy(*weave_views(z2_bf[:], z2_rows[:]))
+            z2_codes = sb(f"z2_codes{c}", [P, width], U32)
+            z2_scales = sb(f"z2_scales{c}", [P, width], U8)
             quantize(z2_codes[:], z2_scales[:], z2_bf[:])
-            out_ps = psum.tile([P, PACK, CHUNK], F32, name=f"out_ps{c}", tag=f"bank{c}")
-            for m in range(PACK):
-                rows = slice(m * P, (m + 1) * P)
-                product(out_ps[:, m, :], w2_codes[:, rows], w2_scales[:, rows], z2_codes[:], z2_scales[:])
-            out_sb = sb(f"out_sb{c}", [P, PACK, CHUNK], F32)
-            nc.vector.tensor_tensor(out_sb[:], out_ps[:], res_t[:, :, cols], ALU.add)
-            nc.sync.dma_start(out_rows[:, :, cols], out_sb[:])
+            return z2_codes, z2_scales
+
+        def last_product(z2_mx, cols, banks, out_tag=None):
+            width = cols.stop - cols.start
+            per_bank = PACK // len(banks)
+            for b, bank in enumerate(banks):
+                blocks = slice(b * per_bank, (b + 1) * per_bank)
+                out_ps = psum.tile([P, per_bank, width], F32, name=f"out_ps{bank}", tag=f"bank{bank}")
+                for m in range(per_bank):
+                    rows = slice((blocks.start + m) * P, (blocks.start + m + 1) * P)
+                    product(out_ps[:, m, :], w2_codes[:, rows], w2_scales[:, rows], z2_mx[0][:], z2_mx[1][:])
+                out_sb = sb(f"out_sb{bank}", [P, per_bank, width], F32, tag=out_tag)
+                nc.vector.tensor_tensor(out_sb[:], out_ps[:], res_t[:, blocks, cols], ALU.add)
+                nc.sync.dma_start(out_rows[:, blocks, cols], out_sb[:])
+
+        first, middle, last = slice(0, 256), slice(256, 384), slice(384, 512)
+        last_product(second_difference(0, first, None), first, (0, 1))
+        middle_mx = second_difference(1, middle, "gp_t")
+        last_mx = second_difference(2, last, "hg0")
+        last_product(middle_mx, middle, (2,), "z2_bf2")
+        last_product(last_mx, last, (3, 4))

@@ -19,7 +19,6 @@ P = 128
 PACK = 4
 HALF = 256
 Z_SPLIT = 320
-W2_SPLIT = 384
 
 
 def tile_picked_tok2folddif_none_p_kernel(
@@ -52,6 +51,11 @@ def tile_picked_tok2folddif_none_p_kernel(
                 src.rearrange("p j (c i) -> p c j i", i=PACK),
             )
 
+        warm_in = sb("warm_in", [P, 1], F32)
+        warm_out = sb("warm_out", [P, 1], F32)
+        nc.gpsimd.memset(warm_in[:], 0.0)
+        nc.scalar.activation(warm_out[:], warm_in[:], ACT.Sigmoid)
+
         xw = sb("xw", [P, T], U32)
         xs = sb("xs", [P, T], U8)
         xs_in = sb("xs_in", [P, T], U8)
@@ -76,13 +80,14 @@ def tile_picked_tok2folddif_none_p_kernel(
         n3_t = lists.tile([P, H // 16], U16, name="n3_t")
         nc.sync.dma_start(n1_t[:], n1)
         nc.sync.dma_start(n2_t[:], n2)
-        w2_raw = sb("w2_raw", [P, PACK, N], F32)
-        nc.sync.dma_start(w2_raw[:], rows4(w2))
+        w1_raw = [sb(f"w1_raw{h}", [P, PACK, HALF], F32) for h in range(2)]
+        for h in range(2):
+            nc.sync.dma_start(w1_raw[h][:], rows4(w1)[:, :, h * HALF : (h + 1) * HALF])
         nc.sync.dma_start(gt_t[:], gt.rearrange("(p j) o -> p (j o)", j=PACK))
-        w1_raw = sb("w1_raw", [P, PACK, H], F32)
-        nc.sync.dma_start(w1_raw[:], rows4(w1))
         nc.sync.dma_start(n3_t[:], n3)
         nc.sync.dma_start(gp_t[:], gp.rearrange("(p j) o -> p (j o)", j=PACK))
+        w2_raw = sb("w2_raw", [P, PACK, N], F32)
+        nc.sync.dma_start(w2_raw[:], rows4(w2))
         res_t = sb("res_t", [P, PACK, H], F32)
         nc.sync.dma_start(res_t[:], res.rearrange("(m p) c -> p m c", p=P))
 
@@ -110,33 +115,42 @@ def tile_picked_tok2folddif_none_p_kernel(
                 product(y_ps[t][:, h * HALF : (h + 1) * HALF], tok_words[:, cols], tok_scales[:, cols],
                         wa_mx[h][0][:], wa_mx[h][1][:])
 
-        ds = [sb(f"ds{t}", [P, H], F32) for t in range(PACK)]
-        for t in range(3):
-            nc.vector.tensor_copy(ds[t][:], y_ps[t][:])
-        for t in range(PACK):
-            pa = sb(f"pa{t}", [P, W], F32)
-            sig = sb(f"sig{t}", [P, W], F32)
-            nc.scalar.activation(sig[:], ds[t][:].indirect(n2_t[:]), ACT.Sigmoid)
-            nc.scalar.activation(pa[:], ds[t][:].indirect(n1_t[:]), ACT.Copy)
-            if t == 0:
-                nc.scalar.copy(ds[3][:], y_ps[3][:])
-            nc.vector.tensor_tensor(ds[t][:].indirect(n2_t[:]), pa[:], sig[:], ALU.mult)
+        w1_bf = sb("w1_bf", [P, PACK * H], BF16)
+        w1_dealt = w1_bf[:].rearrange("p (t m j) -> p m j t", t=PACK, j=PACK)
+        w1_cols = [w1_raw[h][:].rearrange("p j (m t) -> p m j t", t=PACK) for h in range(2)]
+        nc.scalar.copy(w1_dealt[:, 0:64], w1_cols[0])
+        nc.scalar.copy(w1_dealt[:, 64:128], w1_cols[1])
 
-        w1_bf = sb("w1_bf", [P, PACK * H], BF16, tag="pa1")
-        nc.scalar.copy(
-            w1_bf[:].rearrange("p (t m j) -> p m j t", t=PACK, j=PACK),
-            w1_raw[:].rearrange("p j (m t) -> p m j t", t=PACK),
-        )
-        z_rows = sb("z_rows", [P, PACK, H], BF16, tag="sig1")
-        nc.vector.tensor_scalar(z_rows[:, 3, :], ds[3][:], gt_t[:, 3:4], None, ALU.mult)
-        for t in range(3):
-            nc.scalar.activation(z_rows[:, t, :], ds[t][:], ACT.Copy, scale=gt_t[:, t : t + 1])
-        w1_codes = sb("w1_codes", [P, H], U32)
+        ds = [sb(f"ds{t}", [P, H], F32) for t in range(PACK)]
+        for t in range(PACK):
+            nc.vector.tensor_copy(ds[t][:], y_ps[t][:])
+        pa = [sb(f"pa{t}", [P, W], F32) for t in range(PACK)]
+        sig = [sb(f"sig{t}", [P, W], F32) for t in range(PACK)]
+        for t in range(PACK):
+            nc.scalar.activation(sig[t][:], ds[t][:].indirect(n2_t[:]), ACT.Sigmoid)
+            nc.scalar.activation(pa[t][:], ds[t][:].indirect(n1_t[:]), ACT.Copy)
+
+        def fold_on_vector(t):
+            nc.vector.tensor_tensor(ds[t][:].indirect(n2_t[:]), pa[t][:], sig[t][:], ALU.mult)
+
+        fold_on_vector(0)
+        fold_on_vector(1)
+        ra2 = sb("ra2", [P, W], F32)
+        nc.vector.tensor_tensor(ra2[:], pa[2][:], sig[2][:], ALU.mult)
+        fold_on_vector(3)
+        nc.scalar.activation(ds[2][:].indirect(n2_t[:]), ra2[:], ACT.Copy)
+        w1_codes = sb("w1_codes", [P, H], U32, tag="pa1")
         w1_scales = sb("w1_scales", [P, H], U8)
         quantize(w1_codes[:], w1_scales[:], w1_bf[:])
+        z_rows = sb("z_rows", [P, PACK, H], BF16, tag="sig1")
+        for t in range(PACK):
+            if t % 2 == 0:
+                nc.scalar.activation(z_rows[:, t, :], ds[t][:], ACT.Copy, scale=gt_t[:, t : t + 1])
+            else:
+                nc.vector.tensor_scalar(z_rows[:, t, :], ds[t][:], gt_t[:, t : t + 1], None, ALU.mult)
 
         h_ps = [psum.tile([P, H], F32, name=f"h_ps{t}", tag=f"bank{PACK + t}") for t in range(PACK)]
-        z_bf = sb("z_bf", [P, PACK * H], BF16, tag="pa1")
+        z_bf = sb("z_bf", [P, PACK * H], BF16)
         dst, src = weave_views(z_bf[:, : PACK * Z_SPLIT], z_rows[:, :, :Z_SPLIT])
         nc.vector.tensor_copy(dst, src)
         dst, src = weave_views(z_bf[:, PACK * Z_SPLIT :], z_rows[:, :, Z_SPLIT:])
@@ -153,15 +167,10 @@ def tile_picked_tok2folddif_none_p_kernel(
                 product(h_ps[t][:, h * HALF : (h + 1) * HALF], w1_codes[:, cols], w1_scales[:, cols],
                         z_mx[h][0][:], z_mx[h][1][:])
 
-        w2_codes = sb("w2_codes", [P, N], U32, tag="sig1")
-        w2_scales = sb("w2_scales", [P, N], U8)
-        for part, (cols, tag) in enumerate(((slice(0, W2_SPLIT), "wa_bf1"), (slice(W2_SPLIT, N), "pa1"))):
-            width = cols.stop - cols.start
-            w2_bf = sb(f"w2_bf{part}", [P, width, PACK], BF16, tag=tag)
-            nc.gpsimd.tensor_scalar(
-                w2_bf[:], w2_raw[:, :, cols].rearrange("p j c -> p c j"), 1.0, 0.0, ALU.mult, ALU.add
-            )
-            quantize(w2_codes[:, cols], w2_scales[:, cols], w2_bf[:].rearrange("p c j -> p (c j)"))
+        w2_bf = []
+        for h, (tag, weave) in enumerate((("sig1", nc.scalar.copy), ("z_bf", nc.vector.tensor_copy))):
+            w2_bf.append(sb(f"w2_bf{h}", [P, PACK * HALF], BF16, tag=tag))
+            weave(*weave_views(w2_bf[h][:], w2_raw[:, :, h * HALF : (h + 1) * HALF]))
 
         hs = [sb(f"hs{t}", [P, H], F32) for t in range(PACK)]
         for t in range(PACK):
@@ -169,6 +178,12 @@ def tile_picked_tok2folddif_none_p_kernel(
                 nc.vector.tensor_scalar(hs[t][:], h_ps[t][:], gp_t[:, t : t + 1], None, ALU.mult)
             else:
                 nc.scalar.activation(hs[t][:], h_ps[t][:], ACT.Copy, scale=gp_t[:, t : t + 1])
+
+        w2_codes = sb("w2_codes", [P, N], U32)
+        w2_scales = sb("w2_scales", [P, N], U8)
+        for h in range(2):
+            cols = slice(h * HALF, (h + 1) * HALF)
+            quantize(w2_codes[:, cols], w2_scales[:, cols], w2_bf[h][:])
 
         out_rows = out.rearrange("(m p) c -> p m c", p=P)
         def second_difference(c, cols, hg_tag):

@@ -2,7 +2,7 @@ from contextlib import ExitStack
 
 import concourse.mybir as mybir
 
-K, T, S, N, H, W = 512, 2048, 512, 512, 512, 256
+T, S, N, H, W = 2048, 512, 512, 512, 256
 FLOPS = 3 * 2 * 512 * 512 * 512
 
 F32 = mybir.dt.float32
@@ -17,8 +17,13 @@ ALU = mybir.AluOpType
 
 P = 128
 PACK = 4
+QUADRANT = 32
+SCALE_ROWS = 4
 HALF = 256
+LIST_ROWS = 16
 Z_SPLIT = 320
+RUN_F32 = 2
+RUN_BF16 = 4
 
 
 def tile_picked_tok2folddif_none_p_kernel(
@@ -33,8 +38,11 @@ def tile_picked_tok2folddif_none_p_kernel(
         def sb(name, shape, dtype, tag=None):
             return keep.tile(shape, dtype, name=name, tag=tag or name, align_bytes=64)
 
-        def rows4(w):
-            return w.rearrange("(p j) c -> p j c", j=PACK)
+        def half(h):
+            return slice(h * HALF, (h + 1) * HALF)
+
+        def by_partition(rows):
+            return rows.rearrange("(p j) c -> p j c", j=PACK)
 
         def quantize(codes, scales, values):
             nc.vector.quantize_mx(out=codes.bitcast(FP8X4), scales=scales, in_=values)
@@ -45,104 +53,122 @@ def tile_picked_tok2folddif_none_p_kernel(
                 rhs=rhs.bitcast(FP8X4), rhs_scale=rhs_scales, start=True, stop=True,
             )
 
-        def weave_views(dst, src):
-            return (
-                dst.rearrange("p (c i j) -> p c j i", i=PACK, j=PACK),
-                src.rearrange("p j (c i) -> p c j i", i=PACK),
+        def weave(copy, dst, src, run):
+            copy(
+                dst.rearrange("p (c i j) -> p c j i", i=run, j=PACK),
+                src.rearrange("p j (c i) -> p c j i", i=run),
             )
+
+        def row_tiles(banks, lhs, lhs_scales, rhs_halves):
+            for t in range(PACK):
+                cols = slice(t * P, (t + 1) * P)
+                for h, (rhs, rhs_scales) in enumerate(rhs_halves):
+                    product(banks[t][:, half(h)], lhs[:, cols], lhs_scales[:, cols], rhs[:], rhs_scales[:])
 
         warm_in = sb("warm_in", [P, 1], F32)
         warm_out = sb("warm_out", [P, 1], F32)
         nc.gpsimd.memset(warm_in[:], 0.0)
         nc.scalar.activation(warm_out[:], warm_in[:], ACT.Sigmoid)
 
-        xw = sb("xw", [P, T], U32)
-        xs = sb("xs", [P, T], U8)
-        xs_in = sb("xs_in", [P, T], U8)
-        for q in range(4):
+        table_words = sb("table_words", [P, T], U32)
+        table_scales = sb("table_scales", [P, T], U8)
+        scale_rows = sb("scale_rows", [P, T], U8)
+        live = [slice(QUADRANT * q, QUADRANT * q + SCALE_ROWS) for q in range(P // QUADRANT)]
+        for q, rows in enumerate(live):
             nc.sync.dma_start(
-                xs_in[32 * q : 32 * q + 4, :].bitcast(I32), x_scales[0, 4 * q : 4 * q + 4, :].bitcast(I32)
+                scale_rows[rows, :].bitcast(I32), x_scales[0, SCALE_ROWS * q : SCALE_ROWS * (q + 1), :].bitcast(I32)
             )
-        nc.sync.dma_start(xw[:].bitcast(I32), x_words[0].rearrange("p c r -> p (c r)").bitcast(I32))
-        offs_t = lists.tile([P, S // 16], U16, name="offs_t")
+        nc.sync.dma_start(table_words[:].bitcast(I32), x_words[0].rearrange("p c r -> p (c r)").bitcast(I32))
+        offs_t = lists.tile([P, S // LIST_ROWS], U16, name="offs_t")
         nc.sync.dma_start(offs_t[:], offs)
-        nc.vector.memset(xs[:].bitcast(I32), 0)
-        for q in range(4):
-            rows = slice(32 * q, 32 * q + 4)
-            nc.vector.tensor_copy(xs[rows, :].bitcast(I32), xs_in[rows, :].bitcast(I32))
+        nc.vector.memset(table_scales[:].bitcast(I32), 0)
+        for rows in live:
+            nc.vector.tensor_copy(table_scales[rows, :].bitcast(I32), scale_rows[rows, :].bitcast(I32))
         wa_raw = [sb(f"wa_raw{h}", [P, PACK, HALF], F32) for h in range(2)]
         for h in range(2):
-            nc.sync.dma_start(wa_raw[h][:], rows4(wa)[:, :, h * HALF : (h + 1) * HALF])
+            nc.sync.dma_start(wa_raw[h][:], by_partition(wa)[:, :, half(h)])
         gt_t = sb("gt_t", [P, PACK], F32)
         gp_t = sb("gp_t", [P, PACK], F32)
-        n1_t = lists.tile([P, W // 16], U16, name="n1_t")
-        n2_t = lists.tile([P, W // 16], U16, name="n2_t")
-        n3_t = lists.tile([P, H // 16], U16, name="n3_t")
+        n1_t = lists.tile([P, W // LIST_ROWS], U16, name="n1_t")
+        n2_t = lists.tile([P, W // LIST_ROWS], U16, name="n2_t")
+        n3_t = lists.tile([P, H // LIST_ROWS], U16, name="n3_t")
         nc.sync.dma_start(n1_t[:], n1)
         nc.sync.dma_start(n2_t[:], n2)
         w1_raw = [sb(f"w1_raw{h}", [P, PACK, HALF], F32) for h in range(2)]
         for h in range(2):
-            nc.sync.dma_start(w1_raw[h][:], rows4(w1)[:, :, h * HALF : (h + 1) * HALF])
+            nc.sync.dma_start(w1_raw[h][:], by_partition(w1)[:, :, half(h)])
         nc.sync.dma_start(gt_t[:], gt.rearrange("(p j) o -> p (j o)", j=PACK))
         nc.sync.dma_start(n3_t[:], n3)
         nc.sync.dma_start(gp_t[:], gp.rearrange("(p j) o -> p (j o)", j=PACK))
         w2_raw = sb("w2_raw", [P, PACK, N], F32)
-        nc.sync.dma_start(w2_raw[:], rows4(w2))
+        nc.sync.dma_start(w2_raw[:], by_partition(w2))
         res_t = sb("res_t", [P, PACK, H], F32)
         nc.sync.dma_start(res_t[:], res.rearrange("(m p) c -> p m c", p=P))
 
+        picked_scales = sb("picked_scales", [P, S], U8)
+        picked_words = sb("picked_words", [P, S], U32)
+        nc.vector.tensor_copy(picked_scales[:], table_scales[:].indirect(offs_t[:]))
+        nc.vector.tensor_copy(picked_words[:], table_words[:].indirect(offs_t[:]))
         tok_scales = sb("tok_scales", [P, S], U8)
         tok_words = sb("tok_words", [P, S], U32)
-        nc.vector.tensor_copy(tok_scales[:].rearrange("p (t m) -> p m t", t=PACK), xs[:].indirect(offs_t[:]))
-        nc.vector.tensor_copy(tok_words[:].rearrange("p (t m) -> p m t", t=PACK), xw[:].indirect(offs_t[:]))
+        nc.vector.tensor_copy(
+            tok_words[:].rearrange("p (t m) -> p m t", t=PACK), picked_words[:].rearrange("p (m t) -> p m t", t=PACK)
+        )
+        nc.vector.tensor_copy(
+            tok_scales[:].rearrange("p (t m) -> p t m", t=PACK), picked_scales[:].rearrange("p (m t) -> p t m", t=PACK)
+        )
 
         y_ps = [psum.tile([P, H], F32, name=f"y_ps{t}", tag=f"bank{t}") for t in range(PACK)]
         wa_mx = []
-        for h in range(2):
+        for h, copy in enumerate((nc.scalar.copy, nc.vector.tensor_copy)):
             wa_bf = sb(f"wa_bf{h}", [P, PACK * HALF], BF16)
-            dst, src = weave_views(wa_bf[:], wa_raw[h][:])
-            if h == 0:
-                nc.scalar.copy(dst, src)
-            else:
-                nc.vector.tensor_copy(dst, src)
+            weave(copy, wa_bf[:], wa_raw[h][:], RUN_F32)
             wa_codes = sb(f"wa_codes{h}", [P, HALF], U32)
             wa_scales = sb(f"wa_scales{h}", [P, HALF], U8)
             quantize(wa_codes[:], wa_scales[:], wa_bf[:])
             wa_mx.append((wa_codes, wa_scales))
-        for t in range(PACK):
-            cols = slice(t * P, (t + 1) * P)
-            for h in range(2):
-                product(y_ps[t][:, h * HALF : (h + 1) * HALF], tok_words[:, cols], tok_scales[:, cols],
-                        wa_mx[h][0][:], wa_mx[h][1][:])
+        row_tiles(y_ps, tok_words, tok_scales, wa_mx)
 
-        w1_bf = sb("w1_bf", [P, PACK * H], BF16)
-        w1_dealt = w1_bf[:].rearrange("p (t m j) -> p m j t", t=PACK, j=PACK)
-        w1_cols = [w1_raw[h][:].rearrange("p j (m t) -> p m j t", t=PACK) for h in range(2)]
-        nc.scalar.copy(w1_dealt[:, 0:64], w1_cols[0])
-        nc.scalar.copy(w1_dealt[:, 64:128], w1_cols[1])
+        def deal_w1(pair, tag, copy):
+            dealt = sb(f"w1_bf{pair}", [P, 2, P, PACK], BF16, tag=tag)
+            places = HALF // PACK
+            for h in range(2):
+                copy(
+                    dealt[:, :, places * h : places * (h + 1), :].rearrange("p t m j -> p m j t"),
+                    w1_raw[h][:].rearrange("p j (m t) -> p m j t", t=PACK)[:, :, :, 2 * pair : 2 * pair + 2],
+                )
+            return dealt
+
+        w1_bf = [deal_w1(0, None, nc.scalar.copy)]
 
         ds = [sb(f"ds{t}", [P, H], F32) for t in range(PACK)]
         for t in range(PACK):
             nc.vector.tensor_copy(ds[t][:], y_ps[t][:])
+        w1_bf.append(deal_w1(1, "wa_codes1", nc.vector.tensor_copy))
         pa = [sb(f"pa{t}", [P, W], F32) for t in range(PACK)]
-        sig = [sb(f"sig{t}", [P, W], F32) for t in range(PACK)]
+        gate = [sb(f"gate{t}", [P, W], F32) for t in range(PACK)]
         for t in range(PACK):
-            nc.scalar.activation(sig[t][:], ds[t][:].indirect(n2_t[:]), ACT.Sigmoid)
+            nc.scalar.activation(gate[t][:], ds[t][:].indirect(n2_t[:]), ACT.Sigmoid)
             nc.scalar.activation(pa[t][:], ds[t][:].indirect(n1_t[:]), ACT.Copy)
 
         def fold_on_vector(t):
-            nc.vector.tensor_tensor(ds[t][:].indirect(n2_t[:]), pa[t][:], sig[t][:], ALU.mult)
+            nc.vector.tensor_tensor(ds[t][:].indirect(n2_t[:]), pa[t][:], gate[t][:], ALU.mult)
 
         fold_on_vector(0)
         fold_on_vector(1)
         ra2 = sb("ra2", [P, W], F32)
-        nc.vector.tensor_tensor(ra2[:], pa[2][:], sig[2][:], ALU.mult)
+        nc.vector.tensor_tensor(ra2[:], pa[2][:], gate[2][:], ALU.mult)
         fold_on_vector(3)
         nc.scalar.activation(ds[2][:].indirect(n2_t[:]), ra2[:], ACT.Copy)
+
         w1_codes = sb("w1_codes", [P, H], U32, tag="pa1")
         w1_scales = sb("w1_scales", [P, H], U8)
-        quantize(w1_codes[:], w1_scales[:], w1_bf[:])
-        z_rows = sb("z_rows", [P, PACK, H], BF16, tag="sig1")
+        for pair in range(2):
+            quantize(
+                w1_codes[:, half(pair)], w1_scales[:, half(pair)], w1_bf[pair][:].rearrange("p t m j -> p (t m j)")
+            )
+
+        z_rows = sb("z_rows", [P, PACK, H], BF16, tag="gate1")
         for t in range(PACK):
             if t % 2 == 0:
                 nc.scalar.activation(z_rows[:, t, :], ds[t][:], ACT.Copy, scale=gt_t[:, t : t + 1])
@@ -151,58 +177,51 @@ def tile_picked_tok2folddif_none_p_kernel(
 
         h_ps = [psum.tile([P, H], F32, name=f"h_ps{t}", tag=f"bank{PACK + t}") for t in range(PACK)]
         z_bf = sb("z_bf", [P, PACK * H], BF16)
-        dst, src = weave_views(z_bf[:, : PACK * Z_SPLIT], z_rows[:, :, :Z_SPLIT])
-        nc.vector.tensor_copy(dst, src)
-        dst, src = weave_views(z_bf[:, PACK * Z_SPLIT :], z_rows[:, :, Z_SPLIT:])
-        nc.scalar.copy(dst, src)
+        weave(nc.vector.tensor_copy, z_bf[:, : PACK * Z_SPLIT], z_rows[:, :, :Z_SPLIT], RUN_BF16)
+        weave(nc.scalar.copy, z_bf[:, PACK * Z_SPLIT :], z_rows[:, :, Z_SPLIT:], RUN_BF16)
         z_mx = []
         for h in range(2):
             z_codes = sb(f"z_codes{h}", [P, HALF], U32)
             z_scales = sb(f"z_scales{h}", [P, HALF], U8)
             quantize(z_codes[:], z_scales[:], z_bf[:, h * PACK * HALF : (h + 1) * PACK * HALF])
             z_mx.append((z_codes, z_scales))
-        for t in range(PACK):
-            cols = slice(t * P, (t + 1) * P)
-            for h in range(2):
-                product(h_ps[t][:, h * HALF : (h + 1) * HALF], w1_codes[:, cols], w1_scales[:, cols],
-                        z_mx[h][0][:], z_mx[h][1][:])
+        row_tiles(h_ps, w1_codes, w1_scales, z_mx)
 
         w2_bf = []
-        for h, (tag, weave) in enumerate((("sig1", nc.scalar.copy), ("z_bf", nc.vector.tensor_copy))):
+        for h, (tag, copy) in enumerate((("gate1", nc.scalar.copy), ("z_bf", nc.vector.tensor_copy))):
             w2_bf.append(sb(f"w2_bf{h}", [P, PACK * HALF], BF16, tag=tag))
-            weave(*weave_views(w2_bf[h][:], w2_raw[:, :, h * HALF : (h + 1) * HALF]))
+            weave(copy, w2_bf[h][:], w2_raw[:, :, half(h)], RUN_F32)
 
-        hs = [sb(f"hs{t}", [P, H], F32) for t in range(PACK)]
+        gh = [sb(f"gh{t}", [P, H], F32) for t in range(PACK)]
         for t in range(PACK):
-            if t != 1:
-                nc.vector.tensor_scalar(hs[t][:], h_ps[t][:], gp_t[:, t : t + 1], None, ALU.mult)
+            if t == 1:
+                nc.scalar.activation(gh[t][:], h_ps[t][:], ACT.Copy, scale=gp_t[:, t : t + 1])
             else:
-                nc.scalar.activation(hs[t][:], h_ps[t][:], ACT.Copy, scale=gp_t[:, t : t + 1])
+                nc.vector.tensor_scalar(gh[t][:], h_ps[t][:], gp_t[:, t : t + 1], None, ALU.mult)
 
         w2_codes = sb("w2_codes", [P, N], U32)
         w2_scales = sb("w2_scales", [P, N], U8)
         for h in range(2):
-            cols = slice(h * HALF, (h + 1) * HALF)
-            quantize(w2_codes[:, cols], w2_scales[:, cols], w2_bf[h][:])
+            quantize(w2_codes[:, half(h)], w2_scales[:, half(h)], w2_bf[h][:])
 
         out_rows = out.rearrange("(m p) c -> p m c", p=P)
-        def second_difference(c, cols, hg_tag):
+
+        def difference(name, cols, fetched_tag):
             width = cols.stop - cols.start
-            hg = sb(f"hg{c}", [P, PACK, width], F32, tag=hg_tag)
-            z2_rows = sb(f"z2_rows{c}", [P, PACK, width], BF16)
+            entries = n3_t[:, cols.start // LIST_ROWS : cols.stop // LIST_ROWS]
+            fetched = sb(f"fetched_{name}", [P, PACK, width], F32, tag=fetched_tag)
+            z2_rows = sb(f"z2_rows_{name}", [P, PACK, width], BF16)
             for t in range(PACK):
-                nc.scalar.activation(
-                    hg[:, t, :], hs[t][:].indirect(n3_t[:, cols.start // 16 : cols.stop // 16]), ACT.Copy
-                )
-                nc.vector.tensor_tensor(z2_rows[:, t, :], hs[t][:, cols], hg[:, t, :], ALU.subtract)
-            z2_bf = sb(f"z2_bf{c}", [P, PACK * width], BF16)
-            nc.vector.tensor_copy(*weave_views(z2_bf[:], z2_rows[:]))
-            z2_codes = sb(f"z2_codes{c}", [P, width], U32)
-            z2_scales = sb(f"z2_scales{c}", [P, width], U8)
+                nc.scalar.activation(fetched[:, t, :], gh[t][:].indirect(entries), ACT.Copy)
+                nc.vector.tensor_tensor(z2_rows[:, t, :], gh[t][:, cols], fetched[:, t, :], ALU.subtract)
+            z2_bf = sb(f"z2_bf_{name}", [P, PACK * width], BF16)
+            weave(nc.vector.tensor_copy, z2_bf[:], z2_rows[:], RUN_BF16)
+            z2_codes = sb(f"z2_codes_{name}", [P, width], U32)
+            z2_scales = sb(f"z2_scales_{name}", [P, width], U8)
             quantize(z2_codes[:], z2_scales[:], z2_bf[:])
             return z2_codes, z2_scales
 
-        def last_product(z2_mx, cols, banks, out_tag=None):
+        def last_product(z2_mx, cols, banks, sum_tag=None):
             width = cols.stop - cols.start
             per_bank = PACK // len(banks)
             for b, bank in enumerate(banks):
@@ -211,13 +230,13 @@ def tile_picked_tok2folddif_none_p_kernel(
                 for m in range(per_bank):
                     rows = slice((blocks.start + m) * P, (blocks.start + m + 1) * P)
                     product(out_ps[:, m, :], w2_codes[:, rows], w2_scales[:, rows], z2_mx[0][:], z2_mx[1][:])
-                out_sb = sb(f"out_sb{bank}", [P, per_bank, width], F32, tag=out_tag)
+                out_sb = sb(f"out_sb{bank}", [P, per_bank, width], F32, tag=sum_tag)
                 nc.vector.tensor_tensor(out_sb[:], out_ps[:], res_t[:, blocks, cols], ALU.add)
                 nc.sync.dma_start(out_rows[:, blocks, cols], out_sb[:])
 
-        first, middle, last = slice(0, 256), slice(256, 384), slice(384, 512)
-        last_product(second_difference(0, first, None), first, (0, 1))
-        middle_mx = second_difference(1, middle, "gp_t")
-        last_mx = second_difference(2, last, "hg0")
-        last_product(middle_mx, middle, (2,), "z2_bf2")
+        first, middle, last = slice(0, HALF), slice(HALF, HALF + P), slice(HALF + P, H)
+        last_product(difference("first", first, None), first, (0, 1))
+        middle_mx = difference("middle", middle, "gp_t")
+        last_mx = difference("last", last, "fetched_first")
+        last_product(middle_mx, middle, (2,), "z2_bf_last")
         last_product(last_mx, last, (3, 4))

@@ -65,11 +65,6 @@ def tile_picked_tok2folddif_none_p_kernel(
                 for h, (rhs, rhs_scales) in enumerate(rhs_halves):
                     product(banks[t][:, half(h)], lhs[:, cols], lhs_scales[:, cols], rhs[:], rhs_scales[:])
 
-        warm_in = sb("warm_in", [P, 1], F32)
-        warm_out = sb("warm_out", [P, 1], F32)
-        nc.gpsimd.memset(warm_in[:], 0.0)
-        nc.scalar.activation(warm_out[:], warm_in[:], ACT.Sigmoid)
-
         table_words = sb("table_words", [P, T], U32)
         table_scales = sb("table_scales", [P, T], U8)
         scale_rows = sb("scale_rows", [P, T], U8)

from contextlib import ExitStack

import concourse.mybir as mybir

T, S, N, H, W = 2048, 512, 512, 512, 256
FLOPS = 3 * 2 * 512 * 512 * 512

F32 = mybir.dt.float32
BF16 = mybir.dt.bfloat16
I32 = mybir.dt.int32
U32 = mybir.dt.uint32
U16 = mybir.dt.uint16
U8 = mybir.dt.uint8
FP8X4 = mybir.dt.float8_e4m3fn_x4
ACT = mybir.ActivationFunctionType
ALU = mybir.AluOpType

P = 128
PACK = 4
QUADRANT = 32
SCALE_ROWS = 4
HALF = 256
LIST_ROWS = 16
Z_SPLIT = 320
RUN_F32 = 2
RUN_BF16 = 4


def tile_picked_tok2folddif_none_p_kernel(
    tc, x_words, x_scales, wa, gt, w1, gp, res, w2, offs, n1, n2, n3, out
):
    nc = tc.nc
    with ExitStack() as ctx:
        lists = ctx.enter_context(tc.tile_pool(name="lists", bufs=1))
        keep = ctx.enter_context(tc.tile_pool(name="keep", bufs=1))
        psum = ctx.enter_context(tc.psum_pool(name="psum", bufs=1))

        def sb(name, shape, dtype, tag=None):
            return keep.tile(shape, dtype, name=name, tag=tag or name, align_bytes=64)

        def half(h):
            return slice(h * HALF, (h + 1) * HALF)

        def by_partition(rows):
            return rows.rearrange("(p j) c -> p j c", j=PACK)

        def quantize(codes, scales, values):
            nc.vector.quantize_mx(out=codes.bitcast(FP8X4), scales=scales, in_=values)

        def product(acc, lhs, lhs_scales, rhs, rhs_scales):
            nc.tensor.matmul_mx(
                out=acc, lhsT=lhs.bitcast(FP8X4), lhsT_scale=lhs_scales,
                rhs=rhs.bitcast(FP8X4), rhs_scale=rhs_scales, start=True, stop=True,
            )

        def weave(copy, dst, src, run):
            copy(
                dst.rearrange("p (c i j) -> p c j i", i=run, j=PACK),
                src.rearrange("p j (c i) -> p c j i", i=run),
            )

        def row_tiles(banks, lhs, lhs_scales, rhs_halves):
            for t in range(PACK):
                cols = slice(t * P, (t + 1) * P)
                for h, (rhs, rhs_scales) in enumerate(rhs_halves):
                    product(banks[t][:, half(h)], lhs[:, cols], lhs_scales[:, cols], rhs[:], rhs_scales[:])

        table_words = sb("table_words", [P, T], U32)
        table_scales = sb("table_scales", [P, T], U8)
        scale_rows = sb("scale_rows", [P, T], U8)
        live = [slice(QUADRANT * q, QUADRANT * q + SCALE_ROWS) for q in range(P // QUADRANT)]
        for q, rows in enumerate(live):
            nc.sync.dma_start(
                scale_rows[rows, :].bitcast(I32), x_scales[0, SCALE_ROWS * q : SCALE_ROWS * (q + 1), :].bitcast(I32)
            )
        nc.sync.dma_start(table_words[:].bitcast(I32), x_words[0].rearrange("p c r -> p (c r)").bitcast(I32))
        offs_t = lists.tile([P, S // LIST_ROWS], U16, name="offs_t")
        nc.sync.dma_start(offs_t[:], offs)
        nc.vector.memset(table_scales[:].bitcast(I32), 0)
        for rows in live:
            nc.vector.tensor_copy(table_scales[rows, :].bitcast(I32), scale_rows[rows, :].bitcast(I32))
        wa_raw = [sb(f"wa_raw{h}", [P, PACK, HALF], F32) for h in range(2)]
        for h in range(2):
            nc.sync.dma_start(wa_raw[h][:], by_partition(wa)[:, :, half(h)])
        gt_t = sb("gt_t", [P, PACK], F32)
        gp_t = sb("gp_t", [P, PACK], F32)
        n1_t = lists.tile([P, W // LIST_ROWS], U16, name="n1_t")
        n2_t = lists.tile([P, W // LIST_ROWS], U16, name="n2_t")
        n3_t = lists.tile([P, H // LIST_ROWS], U16, name="n3_t")
        nc.sync.dma_start(n1_t[:], n1)
        nc.sync.dma_start(n2_t[:], n2)
        w1_raw = [sb(f"w1_raw{h}", [P, PACK, HALF], F32) for h in range(2)]
        for h in range(2):
            nc.sync.dma_start(w1_raw[h][:], by_partition(w1)[:, :, half(h)])
        nc.sync.dma_start(gt_t[:], gt.rearrange("(p j) o -> p (j o)", j=PACK))
        nc.sync.dma_start(n3_t[:], n3)
        nc.sync.dma_start(gp_t[:], gp.rearrange("(p j) o -> p (j o)", j=PACK))
        w2_raw = sb("w2_raw", [P, PACK, N], F32)
        nc.sync.dma_start(w2_raw[:], by_partition(w2))
        res_t = sb("res_t", [P, PACK, H], F32)
        nc.sync.dma_start(res_t[:], res.rearrange("(m p) c -> p m c", p=P))

        picked_scales = sb("picked_scales", [P, S], U8)
        picked_words = sb("picked_words", [P, S], U32)
        nc.vector.tensor_copy(picked_scales[:], table_scales[:].indirect(offs_t[:]))
        nc.vector.tensor_copy(picked_words[:], table_words[:].indirect(offs_t[:]))
        tok_scales = sb("tok_scales", [P, S], U8)
        tok_words = sb("tok_words", [P, S], U32)
        nc.vector.tensor_copy(
            tok_words[:].rearrange("p (t m) -> p m t", t=PACK), picked_words[:].rearrange("p (m t) -> p m t", t=PACK)
        )
        nc.vector.tensor_copy(
            tok_scales[:].rearrange("p (t m) -> p t m", t=PACK), picked_scales[:].rearrange("p (m t) -> p t m", t=PACK)
        )

        y_ps = [psum.tile([P, H], F32, name=f"y_ps{t}", tag=f"bank{t}") for t in range(PACK)]
        wa_mx = []
        for h, copy in enumerate((nc.scalar.copy, nc.vector.tensor_copy)):
            wa_bf = sb(f"wa_bf{h}", [P, PACK * HALF], BF16)
            weave(copy, wa_bf[:], wa_raw[h][:], RUN_F32)
            wa_codes = sb(f"wa_codes{h}", [P, HALF], U32)
            wa_scales = sb(f"wa_scales{h}", [P, HALF], U8)
            quantize(wa_codes[:], wa_scales[:], wa_bf[:])
            wa_mx.append((wa_codes, wa_scales))
        row_tiles(y_ps, tok_words, tok_scales, wa_mx)

        def deal_w1(pair, tag, copy):
            dealt = sb(f"w1_bf{pair}", [P, 2, P, PACK], BF16, tag=tag)
            places = HALF // PACK
            for h in range(2):
                copy(
                    dealt[:, :, places * h : places * (h + 1), :].rearrange("p t m j -> p m j t"),
                    w1_raw[h][:].rearrange("p j (m t) -> p m j t", t=PACK)[:, :, :, 2 * pair : 2 * pair + 2],
                )
            return dealt

        w1_bf = [deal_w1(0, None, nc.scalar.copy)]

        ds = [sb(f"ds{t}", [P, H], F32) for t in range(PACK)]
        for t in range(PACK):
            nc.vector.tensor_copy(ds[t][:], y_ps[t][:])
        w1_bf.append(deal_w1(1, "wa_codes1", nc.vector.tensor_copy))
        pa = [sb(f"pa{t}", [P, W], F32) for t in range(PACK)]
        gate = [sb(f"gate{t}", [P, W], F32) for t in range(PACK)]
        for t in range(PACK):
            nc.scalar.activation(gate[t][:], ds[t][:].indirect(n2_t[:]), ACT.Sigmoid)
            nc.scalar.activation(pa[t][:], ds[t][:].indirect(n1_t[:]), ACT.Copy)

        def fold_on_vector(t):
            nc.vector.tensor_tensor(ds[t][:].indirect(n2_t[:]), pa[t][:], gate[t][:], ALU.mult)

        fold_on_vector(0)
        fold_on_vector(1)
        ra2 = sb("ra2", [P, W], F32)
        nc.vector.tensor_tensor(ra2[:], pa[2][:], gate[2][:], ALU.mult)
        fold_on_vector(3)
        nc.scalar.activation(ds[2][:].indirect(n2_t[:]), ra2[:], ACT.Copy)

        w1_codes = sb("w1_codes", [P, H], U32, tag="pa1")
        w1_scales = sb("w1_scales", [P, H], U8)
        for pair in range(2):
            quantize(
                w1_codes[:, half(pair)], w1_scales[:, half(pair)], w1_bf[pair][:].rearrange("p t m j -> p (t m j)")
            )

        z_rows = sb("z_rows", [P, PACK, H], BF16, tag="gate1")
        for t in range(PACK):
            if t % 2 == 0:
                nc.scalar.activation(z_rows[:, t, :], ds[t][:], ACT.Copy, scale=gt_t[:, t : t + 1])
            else:
                nc.vector.tensor_scalar(z_rows[:, t, :], ds[t][:], gt_t[:, t : t + 1], None, ALU.mult)

        h_ps = [psum.tile([P, H], F32, name=f"h_ps{t}", tag=f"bank{PACK + t}") for t in range(PACK)]
        z_bf = sb("z_bf", [P, PACK * H], BF16)
        weave(nc.vector.tensor_copy, z_bf[:, : PACK * Z_SPLIT], z_rows[:, :, :Z_SPLIT], RUN_BF16)
        weave(nc.scalar.copy, z_bf[:, PACK * Z_SPLIT :], z_rows[:, :, Z_SPLIT:], RUN_BF16)
        z_mx = []
        for h in range(2):
            z_codes = sb(f"z_codes{h}", [P, HALF], U32)
            z_scales = sb(f"z_scales{h}", [P, HALF], U8)
            quantize(z_codes[:], z_scales[:], z_bf[:, h * PACK * HALF : (h + 1) * PACK * HALF])
            z_mx.append((z_codes, z_scales))
        row_tiles(h_ps, w1_codes, w1_scales, z_mx)

        w2_bf = []
        for h, (tag, copy) in enumerate((("gate1", nc.scalar.copy), ("z_bf", nc.vector.tensor_copy))):
            w2_bf.append(sb(f"w2_bf{h}", [P, PACK * HALF], BF16, tag=tag))
            weave(copy, w2_bf[h][:], w2_raw[:, :, half(h)], RUN_F32)

        gh = [sb(f"gh{t}", [P, H], F32) for t in range(PACK)]
        for t in range(PACK):
            if t == 1:
                nc.scalar.activation(gh[t][:], h_ps[t][:], ACT.Copy, scale=gp_t[:, t : t + 1])
            else:
                nc.vector.tensor_scalar(gh[t][:], h_ps[t][:], gp_t[:, t : t + 1], None, ALU.mult)

        w2_codes = sb("w2_codes", [P, N], U32)
        w2_scales = sb("w2_scales", [P, N], U8)
        for h in range(2):
            quantize(w2_codes[:, half(h)], w2_scales[:, half(h)], w2_bf[h][:])

        out_rows = out.rearrange("(m p) c -> p m c", p=P)

        def difference(name, cols, fetched_tag):
            width = cols.stop - cols.start
            entries = n3_t[:, cols.start // LIST_ROWS : cols.stop // LIST_ROWS]
            fetched = sb(f"fetched_{name}", [P, PACK, width], F32, tag=fetched_tag)
            z2_rows = sb(f"z2_rows_{name}", [P, PACK, width], BF16)
            for t in range(PACK):
                nc.scalar.activation(fetched[:, t, :], gh[t][:].indirect(entries), ACT.Copy)
                nc.vector.tensor_tensor(z2_rows[:, t, :], gh[t][:, cols], fetched[:, t, :], ALU.subtract)
            z2_bf = sb(f"z2_bf_{name}", [P, PACK * width], BF16)
            weave(nc.vector.tensor_copy, z2_bf[:], z2_rows[:], RUN_BF16)
            z2_codes = sb(f"z2_codes_{name}", [P, width], U32)
            z2_scales = sb(f"z2_scales_{name}", [P, width], U8)
            quantize(z2_codes[:], z2_scales[:], z2_bf[:])
            return z2_codes, z2_scales

        def last_product(z2_mx, cols, banks, sum_tag=None):
            width = cols.stop - cols.start
            per_bank = PACK // len(banks)
            for b, bank in enumerate(banks):
                blocks = slice(b * per_bank, (b + 1) * per_bank)
                out_ps = psum.tile([P, per_bank, width], F32, name=f"out_ps{bank}", tag=f"bank{bank}")
                for m in range(per_bank):
                    rows = slice((blocks.start + m) * P, (blocks.start + m + 1) * P)
                    product(out_ps[:, m, :], w2_codes[:, rows], w2_scales[:, rows], z2_mx[0][:], z2_mx[1][:])
                out_sb = sb(f"out_sb{bank}", [P, per_bank, width], F32, tag=sum_tag)
                nc.vector.tensor_tensor(out_sb[:], out_ps[:], res_t[:, blocks, cols], ALU.add)
                nc.sync.dma_start(out_rows[:, blocks, cols], out_sb[:])

        first, middle, last = slice(0, HALF), slice(HALF, HALF + P), slice(HALF + P, H)
        last_product(difference("first", first, None), first, (0, 1))
        middle_mx = difference("middle", middle, "gp_t")
        last_mx = difference("last", last, "fetched_first")
        last_product(middle_mx, middle, (2,), "z2_bf_last")
        last_product(last_mx, last, (3, 4))
